import numpy as np
import ml_dtypes


def mxq(x, axis, fmt="e4m3"):
    dtype, down = {"e4m3": (ml_dtypes.float8_e4m3fn, 7), "e5m2": (ml_dtypes.float8_e5m2, 14)}[fmt]
    v = np.moveaxis(np.asarray(x, np.float32).astype(ml_dtypes.bfloat16).astype(np.float64), axis, -1)
    blocks = v.reshape(v.shape[:-1] + (-1, 32))
    amax = np.abs(blocks).max(-1, keepdims=True)
    byte = np.maximum(np.where(amax > 0, np.frexp(amax)[1] - 1 + 127, 0) - down, 1)
    scale = np.exp2(byte - 127.0)
    codes = (blocks / scale).astype(np.float32).astype(dtype).astype(np.float64)
    return np.moveaxis((codes * scale).reshape(v.shape), -1, axis)


WIDE = False


def mx_kscale(k):
    if not WIDE:
        return np.ones(k)
    levels = np.array([10, -10, 5, -5, 0])
    if k % 512:
        return np.exp2(np.random.permutation(np.resize(levels, k // 32))).repeat(32)
    a = np.empty((k // 512, 16))
    for p in range(k // 512):
        a[p, :8] = np.random.permutation(np.resize(levels, 8))
        for g in range(8):
            far = levels[np.abs(levels - a[p, g]) >= 10]
            a[p, g + 8] = far[np.random.randint(len(far))]
    return np.exp2(a.ravel()).repeat(32)


def f64(x):
    return np.asarray(x).astype(np.float64)


def striped(idx):
    return np.tile(idx.reshape(-1, 16).T, (8, 1)).astype(np.uint16)


def unstriped(offs):
    return offs[:16].T.reshape(-1).astype(np.int64)


def striped8(idx):
    return np.concatenate([x.reshape(-1, 16).T for x in idx]).astype(np.uint16)


def runs(offs, k):
    lists = np.stack([offs[16 * r : 16 * r + 16].T.reshape(-1) for r in range(8)]).astype(np.int64)
    return lists[np.arange(k) % 512 // 64]


def pack_weight(w):
    k, n = w.shape
    w = f64(np.asarray(w, np.float32).astype(ml_dtypes.bfloat16)).reshape(k // 32, 32, n)
    amax = np.abs(w).max(1)
    byte = np.clip(np.where(amax > 0, np.frexp(amax)[1] - 1 + 127 - 7, 1), 1, 254)
    scaled = (w * np.exp2(127.0 - byte)[:, None, :]).reshape(k, n).astype(np.float32)
    words = np.ascontiguousarray(scaled.reshape(k // 512, 128, 4, n).transpose(0, 1, 3, 2)).astype(ml_dtypes.float8_e4m3fn).view(np.uint8)
    return words, np.ascontiguousarray(byte.astype(np.uint8).reshape(k // 512, 16, n))


def unpack_weight(words, scales):
    g, p, n, _ = words.shape
    vals = np.ascontiguousarray(words).view(ml_dtypes.float8_e4m3fn).astype(np.float64) * np.repeat(np.exp2(scales.astype(np.float64) - 127.0), 8, axis=1)[..., None]
    return vals.transpose(0, 1, 3, 2).reshape(g * 512, n)


def sigmoid(v):
    return 1.0 / (1.0 + np.exp(-np.maximum(v, -700.0)))


K, T, S, H, G, W = 512, 1024, 256, 512, 2048, 128


def setup_inputs():
    n = np.random.standard_normal
    s = mx_kscale(K)[:, None]
    packed_xT = pack_weight(n((K, T)) * s)
    packed_w1 = pack_weight(n((K, H)) / np.sqrt(2 * K) / s)
    packed_w2 = pack_weight(n((K, H)) / np.sqrt(2 * K) / s)
    packed_dT = pack_weight(n((K, G)) / s)
    perm = np.random.permutation(S)
    perm2 = np.random.permutation(S)
    return {
        "x_words": packed_xT[0],
        "x_scales": packed_xT[1],
        "w1_words": packed_w1[0],
        "w1_scales": packed_w1[1],
        "w2_words": packed_w2[0],
        "w2_scales": packed_w2[1],
        "sl": np.random.uniform(1.0, 2.0, (H, 1)).astype(np.float32),
        "th": (0.5 * n((H, 1))).astype(np.float32),
        "gs": (np.random.uniform(0.5, 1.5, (K, 1)) * s).astype(np.float32),
        "d_words": packed_dT[0],
        "d_scales": packed_dT[1],
        "offs": striped(np.random.permutation(T)[:S]),
        "two": striped(np.random.permutation(T)[:S]),
        "n1": striped(np.random.permutation(S)),
        "n2": striped(np.random.permutation(S)),
        "n3": striped(np.random.permutation(S)),
        "k1": striped8(np.random.randint(0, G, (8, H))),
        "k2": striped8(np.random.randint(0, G, (8, H))),
        "hz": striped8(np.random.randint(0, T, (8, S))),
        "n4": striped(perm[:W]),
        "n5": striped(perm[W:]),
        "n6": striped(perm2[:W]),
        "n7": striped(perm2[W:]),
        "n8": striped(np.random.permutation(S)),
    }


def reference(x_words, x_scales, w1_words, w1_scales, w2_words, w2_scales, sl, th, gs, d_words, d_scales, offs, two, n1, n2, n3, k1, k2, hz, n4, n5, n6, n7, n8):
    d_k1 = unpack_weight(d_words, d_scales)[np.arange(K)[:, None], runs(k1, K)]
    xq = unpack_weight(x_words, x_scales)[:, unstriped(offs)]
    x_two = unpack_weight(x_words, x_scales)[:, unstriped(two)]
    y = unpack_weight(w1_words, w1_scales).T @ xq + unpack_weight(w2_words, w2_scales).T @ x_two
    ds2 = np.zeros((H, S))
    ds2[:, unstriped(n2)] = y
    ds = np.zeros((H, S))
    ds[:, unstriped(n1)] = y
    sg = sigmoid(f64(sl) * (ds[:, unstriped(n3)] - f64(th)))
    z = f64(gs) * (ds2 * sg)
    d_k2 = unpack_weight(d_words, d_scales)[np.arange(K)[:, None], runs(k2, K)]
    x_hz = unpack_weight(x_words, x_scales)[np.arange(K)[:, None], runs(hz, K)]
    h2 = 0.0625 * ((d_k1.T @ mxq(z, 0, "e4m3") + d_k2.T @ x_hz))
    pa = h2[:, unstriped(n4)]
    pb = h2[:, unstriped(n5)]
    rb = np.minimum(pa, pb)
    ra = pa - pb
    ua = np.zeros((H, S))
    ua[:, unstriped(n6)] = ra
    ub = ua.copy()
    ub[:, unstriped(n7)] = rb
    return np.maximum(ub, ub[:, unstriped(n8)])

@@ -1,0 +1,267 @@
+from contextlib import ExitStack
+
+import concourse.mybir as mybir
+
+K, T, S, H, G, W = 512, 1024, 256, 512, 2048, 128
+FLOPS = 4 * 2 * K * H * S
+
+F32 = mybir.dt.float32
+BF16 = mybir.dt.bfloat16
+I32 = mybir.dt.int32
+U32 = mybir.dt.uint32
+U16 = mybir.dt.uint16
+U8 = mybir.dt.uint8
+FP8X4 = mybir.dt.float8_e4m3fn_x4
+ALU = mybir.AluOpType
+ACT = mybir.ActivationFunctionType
+
+P = 128
+PACK = 4
+TILES = H // P
+WIDE = 2 * S
+HALF = S // 2
+BANKS = 8
+
+
+def tile_picked_dttzmhesntwcpgf_none_p_kernel(
+    tc, x_words, x_scales, w1_words, w1_scales, w2_words, w2_scales, sl, th, gs, d_words, d_scales,
+    offs, two, n1, n2, n3, k1, k2, hz, n4, n5, n6, n7, n8, out,
+):
+    nc = tc.nc
+    with ExitStack() as ctx:
+        lists = ctx.enter_context(tc.tile_pool(name="lists", bufs=1))
+        keep = ctx.enter_context(tc.tile_pool(name="keep", bufs=1))
+        psum = ctx.enter_context(tc.psum_pool(name="psum", bufs=1))
+
+        def load_list(name, dram):
+            tile = lists.tile(list(dram.shape), U16, name=name)
+            nc.sync.dma_start(tile[:], dram)
+            return tile
+
+        def load_words(name, dram, queue):
+            tile = keep.tile([P, dram.shape[2]], U32, name=name, tag=name, align_bytes=64)
+            queue.dma_start(tile[:].bitcast(I32), dram[0].rearrange("p n t -> p (n t)").bitcast(I32))
+            return tile
+
+        def zeroed_bytes(name, width):
+            tile = keep.tile([P, width], U8, name=name, align_bytes=64)
+            nc.vector.memset(tile[:].bitcast(I32), 0)
+            return tile
+
+        def load_row_values(name, dram):
+            tile = keep.tile([P, PACK], F32, name=name)
+            nc.sync.dma_start(tile[:], dram.rearrange("(p t) o -> p (t o)", t=PACK))
+            return tile
+
+        def gather(dst, window, offsets):
+            nc.vector.tensor_copy(dst, window[:].indirect(offsets[:]))
+
+        x_bytes = keep.tile([P, T], U8, align_bytes=64)
+        w_bytes = keep.tile([P, H], U8, align_bytes=64)
+        d_bytes = zeroed_bytes("d_bytes", G)
+
+        def load_w_scales(j, scales, i):
+            rows = scales[0, i:16:4, :].bitcast(I32)
+            nc.sync.dma_start(
+                w_bytes[4 * j + i : P : 8, :].bitcast(I32), rows.unsqueeze(1).to_broadcast([4, 4, H // 4])
+            )
+
+        offs_t = load_list("offs_t", offs)
+        two_t = load_list("two_t", two)
+        for q in range(4):
+            rows = x_scales[0, 4 * q : 4 * q + 4, :].bitcast(I32)
+            nc.sync.dma_start(
+                x_bytes[32 * q : 32 * q + 32, :].bitcast(I32), rows.unsqueeze(0).to_broadcast([8, 4, T // 4])
+            )
+        w1_w = load_words("w1_w", w1_words, nc.gpsimd)
+        w2_w = load_words("w2_w", w2_words, nc.gpsimd)
+        load_w_scales(0, w1_scales, 0)
+        x_w = load_words("x_w", x_words, nc.sync)
+        for i in range(1, 4):
+            load_w_scales(0, w1_scales, i)
+        for i in range(4):
+            load_w_scales(1, w2_scales, i)
+        n1_t = load_list("n1_t", n1)
+        n2_t = load_list("n2_t", n2)
+        hz_t = load_list("hz_t", hz)
+        k1_t = load_list("k1_t", k1)
+        k2_t = load_list("k2_t", k2)
+        for i in range(2):
+            nc.sync.dma_start(d_bytes[i:P:16, :].bitcast(I32), d_scales[0, i:16:2, :].bitcast(I32))
+        d_w = load_words("d_w", d_words, nc.sync)
+        sl_t = load_row_values("sl_t", sl)
+        th_t = load_row_values("th_t", th)
+        n3_t = load_list("n3_t", n3)
+        gs_t = load_row_values("gs_t", gs)
+        n4_t = load_list("n4_t", n4)
+        n5_t = load_list("n5_t", n5)
+        n6_t = load_list("n6_t", n6)
+        n7_t = load_list("n7_t", n7)
+        n8_t = load_list("n8_t", n8)
+
+        xo_bytes = keep.tile([P, S], U8, align_bytes=64)
+        xt_bytes = keep.tile([P, S], U8, align_bytes=64)
+        xo_w = keep.tile([P, S], U32, align_bytes=64)
+        xt_w = keep.tile([P, S], U32, align_bytes=64)
+        gather(xo_bytes[:], x_bytes, offs_t)
+        gather(xt_bytes[:], x_bytes, two_t)
+        for first in (0, HALF):
+            entries = slice(first // 16, (first + HALF) // 16)
+            gather(xo_w[:, first : first + HALF], x_w, offs_t[:, entries])
+            gather(xt_w[:, first : first + HALF], x_w, two_t[:, entries])
+
+        w1_dealt = keep.tile([P, H], U32, align_bytes=64)
+        w2_dealt = keep.tile([P, H], U32, align_bytes=64)
+        wb_dealt = keep.tile([P, H], U8, align_bytes=64)
+        for dealt, raw, tiles in (
+            (w1_dealt, w1_w, slice(0, TILES)), (w2_dealt, w2_w, slice(0, 1)), (w2_dealt, w2_w, slice(1, TILES)),
+        ):
+            nc.scalar.copy(
+                dealt[:].rearrange("p (t m) -> p t m", t=PACK)[:, tiles, :],
+                raw[:].rearrange("p (m t) -> p t m", t=PACK)[:, tiles, :],
+            )
+        for engine, tiles in ((nc.gpsimd, slice(0, 1)), (nc.vector, slice(1, TILES))):
+            engine.tensor_copy(
+                wb_dealt[:].rearrange("p (t m) -> p t m", t=PACK)[:, tiles, :],
+                w_bytes[:].rearrange("p (m t) -> p t m", t=PACK)[:, tiles, :],
+            )
+
+
+        y = [keep.tile([P, S], F32, name="y%d" % t) for t in range(TILES)]
+        y_pieces = [(0, 0, HALF), (0, HALF, S)] + [(t, 0, S) for t in range(1, TILES)]
+        for bank, (t, first, last) in enumerate(y_pieces):
+            rows = slice(t * P, (t + 1) * P)
+            acc = psum.tile([P, last - first], F32, name="y_acc%d" % bank, tag="bank%d" % bank)
+            nc.tensor.matmul_mx(
+                acc[:], lhsT=w1_dealt[:, rows].bitcast(FP8X4), lhsT_scale=wb_dealt[:, rows],
+                rhs=xo_w[:, first:last].bitcast(FP8X4), rhs_scale=xo_bytes[:, first:last], start=True, stop=False,
+            )
+            nc.tensor.matmul_mx(
+                acc[:], lhsT=w2_dealt[:, rows].bitcast(FP8X4), lhsT_scale=wb_dealt[4:P, rows],
+                rhs=xt_w[:, first:last].bitcast(FP8X4), rhs_scale=xt_bytes[:, first:last], start=False, stop=True,
+            )
+            nc.vector.tensor_copy(y[t][:, first:last], acc[:])
+
+        dk_w = [keep.tile([P, H], U32, name="dk%d_w" % j, align_bytes=64) for j in range(2)]
+        dk_raw = keep.tile([P, 2 * H], U8, align_bytes=64)
+        xh_w = keep.tile([P, S], U32, align_bytes=64)
+        xh_raw = keep.tile([P, S], U8, align_bytes=64)
+        gather(dk_raw[:, H:], d_bytes, k2_t)
+        gather(dk_raw[:, :H], d_bytes, k1_t)
+        gather(xh_raw[:], x_bytes, hz_t)
+        dk_bytes = keep.tile([P, 2 * H], U8, align_bytes=64)
+        xh_bytes = keep.tile([P, S], U8, align_bytes=64)
+        for placed, raw, odd in ((dk_bytes, dk_raw, 16), (xh_bytes, xh_raw, 18)):
+            nc.vector.tensor_copy(placed[:].bitcast(I32), raw[:].bitcast(I32))
+            for i in range(2):
+                nc.sync.dma_start(placed[2 + i : P : 32, :].bitcast(I32), raw[odd + i : P : 32, :].bitcast(I32))
+        gather(dk_w[1][:], d_w, k2_t)
+        gather(xh_w[:], x_w, hz_t)
+        gather(dk_w[0][:], d_w, k1_t)
+
+        bias = keep.tile([P, PACK], F32, tag="d_w", align_bytes=64)
+        nc.vector.scalar_tensor_tensor(bias[:], sl_t[:], -1.0, th_t[:], ALU.mult, ALU.mult)
+
+        h_acc = []
+        for piece, (t, first, last) in enumerate(y_pieces):
+            bank = (len(y_pieces) + piece) % BANKS
+            acc = psum.tile([P, last - first], F32, name="h_acc%d" % piece, tag="bank%d" % bank)
+            nc.tensor.matmul_mx(
+                acc[:], lhsT=dk_w[1][:, t * P : (t + 1) * P].bitcast(FP8X4),
+                lhsT_scale=dk_bytes[:, H + t * P : H + (t + 1) * P],
+                rhs=xh_w[:, first:last].bitcast(FP8X4), rhs_scale=xh_bytes[:, first:last], start=True, stop=False,
+            )
+            h_acc.append(acc)
+
+        ds_tags = ["ds_a", "ds_b", "ds_c", "ds_a"]
+        ds2_tags = ["ds2_a", "ds2_b", "ds2_c", "ds_b"]
+        sg = [keep.tile([P, S], F32, name="sg_%d" % t) for t in range(TILES)]
+        z = keep.tile([P, S, PACK], BF16, align_bytes=64)
+        z_w = keep.tile([P, S], U32, align_bytes=64)
+        z_bytes = keep.tile([P, S], U8, align_bytes=64)
+        ds, ds2 = {}, {}
+
+        def send_ds(t, first=0, last=S):
+            if first == 0:
+                ds[t] = keep.tile([P, WIDE], F32, name="ds_%d" % t, tag=ds_tags[t])
+            nc.scalar.activation(ds[t][:].indirect(n1_t[:, first // 16 : last // 16]), y[t][:, first:last], ACT.Copy)
+
+        def send_ds2(t, first=0, last=S):
+            if first == 0:
+                ds2[t] = keep.tile([P, WIDE], F32, name="ds2_%d" % t, tag=ds2_tags[t])
+            nc.scalar.activation(ds2[t][:].indirect(n2_t[:, first // 16 : last // 16]), y[t][:, first:last], ACT.Copy)
+
+        def gate(t, first, last):
+            nc.scalar.activation(
+                sg[t][:, first:last], ds[t][:].indirect(n3_t[:, first // 16 : last // 16]), ACT.Sigmoid,
+                bias=bias[:, t : t + 1], scale=sl_t[:, t : t + 1],
+            )
+
+        def weigh(t, first, last):
+            nc.vector.scalar_tensor_tensor(
+                z[:, first:last, t], ds2[t][:, first:last], gs_t[:, t : t + 1], sg[t][:, first:last],
+                ALU.mult, ALU.mult,
+            )
+
+        for t, first, last in y_pieces[:-1]:
+            send_ds(t, first, last)
+            send_ds2(t, first, last)
+        gate(0, 0, S)
+        weigh(0, 0, S)
+        gate(1, 0, S)
+        weigh(1, 0, S)
+        send_ds(3)
+        gate(2, 0, S)
+        weigh(2, 0, S)
+        send_ds2(3)
+        for first in (0, HALF):
+            gate(3, first, first + HALF)
+            weigh(3, first, first + HALF)
+        for first in (0, HALF):
+            cols = slice(first, first + HALF)
+            nc.vector.quantize_mx(
+                out=z_w[:, cols].bitcast(FP8X4), scales=z_bytes[:, cols],
+                in_=z[:, cols, :].rearrange("p n t -> p (n t)"),
+            )
+        for piece, (t, first, last) in enumerate(y_pieces):
+            nc.tensor.matmul_mx(
+                h_acc[piece][:], lhsT=dk_w[0][:, t * P : (t + 1) * P].bitcast(FP8X4),
+                lhsT_scale=dk_bytes[:, t * P : (t + 1) * P],
+                rhs=z_w[:, first:last].bitcast(FP8X4), rhs_scale=z_bytes[:, first:last], start=False, stop=True,
+            )
+
+        h2 = [keep.tile([P, S], F32, name="h2_%d" % t) for t in range(TILES)]
+        pa = [keep.tile([P, W], F32, name="pa_%d" % t) for t in range(TILES)]
+        pb = [keep.tile([P, W], F32, name="pb_%d" % t) for t in range(TILES)]
+        ra = [keep.tile([P, W], F32, name="ra_%d" % t) for t in range(TILES)]
+        rb = [keep.tile([P, W], F32, name="rb_%d" % t) for t in range(TILES)]
+        ub = [keep.tile([P, WIDE], F32, name="ub_%d" % t) for t in range(TILES)]
+        far = [keep.tile([P, S], F32, name="far_%d" % t) for t in range(TILES)]
+        res = [keep.tile([P, S], F32, name="res_%d" % t) for t in range(TILES)]
+        for piece, (t, first, last) in enumerate(y_pieces):
+            nc.vector.tensor_scalar(h2[t][:, first:last], h_acc[piece][:], 0.0625, None, ALU.mult)
+
+        def pair_up(t):
+            nc.scalar.activation(pa[t][:], h2[t][:].indirect(n4_t[:]), ACT.Copy)
+            nc.scalar.activation(pb[t][:], h2[t][:].indirect(n5_t[:]), ACT.Copy)
+            nc.vector.tensor_tensor(ra[t][:], pa[t][:], pb[t][:], ALU.subtract)
+            nc.vector.tensor_tensor(rb[t][:], pa[t][:], pb[t][:], ALU.min)
+
+        def share_out(t):
+            nc.scalar.activation(ub[t][:].indirect(n6_t[:]), ra[t][:], ACT.Copy)
+            nc.scalar.activation(ub[t][:].indirect(n7_t[:]), rb[t][:], ACT.Copy)
+
+        def finish(t):
+            for first, last in ((0, HALF), (HALF, S)) if t == TILES - 1 else ((0, S),):
+                entries = n8_t[:, first // 16 : last // 16]
+                nc.scalar.activation(far[t][:, first:last], ub[t][:].indirect(entries), ACT.Copy)
+                nc.vector.tensor_tensor(res[t][:, first:last], ub[t][:, first:last], far[t][:, first:last], ALU.max)
+                nc.sync.dma_start(out[t * P : (t + 1) * P, first:last], res[t][:, first:last])
+
+        for step in range(TILES + 2):
+            if step < TILES:
+                pair_up(step)
+            if 1 <= step <= TILES:
+                share_out(step - 1)
+            if step >= 2:
+                finish(step - 2)

@@ -56,6 +56,11 @@ def tile_picked_dttzmhesntwcpgf_none_p_kernel(
         def gather(dst, window, offsets):
             nc.vector.tensor_copy(dst, window[:].indirect(offsets[:]))
 
+        warm_in = keep.tile([P, 1], F32)
+        warm_out = keep.tile([P, 1], F32)
+        nc.vector.memset(warm_in[:], 0.0)
+        nc.scalar.activation(warm_out[:], warm_in[:], ACT.Sigmoid)
+
         x_bytes = keep.tile([P, T], U8, align_bytes=64)
         w_bytes = keep.tile([P, H], U8, align_bytes=64)
         d_bytes = zeroed_bytes("d_bytes", G)

@@ -43,11 +43,6 @@ def tile_picked_dttzmhesntwcpgf_none_p_kernel(
             queue.dma_start(tile[:].bitcast(I32), dram[0].rearrange("p n t -> p (n t)").bitcast(I32))
             return tile
 
-        def zeroed_bytes(name, width):
-            tile = keep.tile([P, width], U8, name=name, align_bytes=64)
-            nc.vector.memset(tile[:].bitcast(I32), 0)
-            return tile
-
         def load_row_values(name, dram):
             tile = keep.tile([P, PACK], F32, name=name)
             nc.sync.dma_start(tile[:], dram.rearrange("(p t) o -> p (t o)", t=PACK))
@@ -63,7 +58,7 @@ def tile_picked_dttzmhesntwcpgf_none_p_kernel(
 
         x_bytes = keep.tile([P, T], U8, align_bytes=64)
         w_bytes = keep.tile([P, H], U8, align_bytes=64)
-        d_bytes = zeroed_bytes("d_bytes", G)
+        d_bytes = keep.tile([P, G], U8, align_bytes=64)
 
         def load_w_scales(j, scales, i):
             rows = scales[0, i:16:4, :].bitcast(I32)
@@ -92,7 +87,8 @@ def tile_picked_dttzmhesntwcpgf_none_p_kernel(
         k1_t = load_list("k1_t", k1)
         k2_t = load_list("k2_t", k2)
         for i in range(2):
-            nc.sync.dma_start(d_bytes[i:P:16, :].bitcast(I32), d_scales[0, i:16:2, :].bitcast(I32))
+            rows = d_scales[0, i:16:2, :].bitcast(I32)
+            nc.sync.dma_start(d_bytes[i:P:2, :].bitcast(I32), rows.unsqueeze(1).to_broadcast([8, 8, G // 4]))
         d_w = load_words("d_w", d_words, nc.sync)
         sl_t = load_row_values("sl_t", sl)
         th_t = load_row_values("th_t", th)
@@ -145,23 +141,26 @@ def tile_picked_dttzmhesntwcpgf_none_p_kernel(
                 acc[:], lhsT=w2_dealt[:, rows].bitcast(FP8X4), lhsT_scale=wb_dealt[4:P, rows],
                 rhs=xt_w[:, first:last].bitcast(FP8X4), rhs_scale=xt_bytes[:, first:last], start=False, stop=True,
             )
-            nc.vector.tensor_copy(y[t][:, first:last], acc[:])
+            if bank == 0:
+                nc.scalar.copy(y[t][:, first:last], acc[:])
+            else:
+                nc.vector.tensor_copy(y[t][:, first:last], acc[:])
 
         dk_w = [keep.tile([P, H], U32, name="dk%d_w" % j, align_bytes=64) for j in range(2)]
         dk_raw = keep.tile([P, 2 * H], U8, align_bytes=64)
         xh_w = keep.tile([P, S], U32, align_bytes=64)
         xh_raw = keep.tile([P, S], U8, align_bytes=64)
+        gather(xh_raw[:], x_bytes, hz_t)
+        gather(xh_w[:], x_w, hz_t)
         gather(dk_raw[:, H:], d_bytes, k2_t)
         gather(dk_raw[:, :H], d_bytes, k1_t)
-        gather(xh_raw[:], x_bytes, hz_t)
         dk_bytes = keep.tile([P, 2 * H], U8, align_bytes=64)
         xh_bytes = keep.tile([P, S], U8, align_bytes=64)
-        for placed, raw, odd in ((dk_bytes, dk_raw, 16), (xh_bytes, xh_raw, 18)):
+        for placed, raw, odd in ((xh_bytes, xh_raw, 18), (dk_bytes, dk_raw, 16)):
             nc.vector.tensor_copy(placed[:].bitcast(I32), raw[:].bitcast(I32))
             for i in range(2):
-                nc.sync.dma_start(placed[2 + i : P : 32, :].bitcast(I32), raw[odd + i : P : 32, :].bitcast(I32))
+                nc.gpsimd.dma_start(placed[2 + i : P : 32, :].bitcast(I32), raw[odd + i : P : 32, :].bitcast(I32))
         gather(dk_w[1][:], d_w, k2_t)
-        gather(xh_w[:], x_w, hz_t)
         gather(dk_w[0][:], d_w, k1_t)
 
         bias = keep.tile([P, PACK], F32, tag="d_w", align_bytes=64)
@@ -257,7 +256,7 @@ def tile_picked_dttzmhesntwcpgf_none_p_kernel(
             nc.scalar.activation(ub[t][:].indirect(n7_t[:]), rb[t][:], ACT.Copy)
 
         def finish(t):
-            for first, last in ((0, HALF), (HALF, S)) if t == TILES - 1 else ((0, S),):
+            for first, last in ((0, S - 64), (S - 64, S)) if t == TILES - 1 else ((0, S),):
                 entries = n8_t[:, first // 16 : last // 16]
                 nc.scalar.activation(far[t][:, first:last], ub[t][:].indirect(entries), ACT.Copy)
                 nc.vector.tensor_tensor(res[t][:, first:last], ub[t][:, first:last], far[t][:, first:last], ALU.max)

@@ -51,18 +51,13 @@ def tile_picked_dttzmhesntwcpgf_none_p_kernel(
         def gather(dst, window, offsets):
             nc.vector.tensor_copy(dst, window[:].indirect(offsets[:]))
 
-        warm_in = keep.tile([P, 1], F32)
-        warm_out = keep.tile([P, 1], F32)
-        nc.vector.memset(warm_in[:], 0.0)
-        nc.scalar.activation(warm_out[:], warm_in[:], ACT.Sigmoid)
-
         x_bytes = keep.tile([P, T], U8, align_bytes=64)
         w_bytes = keep.tile([P, H], U8, align_bytes=64)
         d_bytes = keep.tile([P, G], U8, align_bytes=64)
 
-        def load_w_scales(j, scales, i):
+        def load_w_scales(j, scales, i, queue):
             rows = scales[0, i:16:4, :].bitcast(I32)
-            nc.sync.dma_start(
+            queue.dma_start(
                 w_bytes[4 * j + i : P : 8, :].bitcast(I32), rows.unsqueeze(1).to_broadcast([4, 4, H // 4])
             )
 
@@ -70,17 +65,23 @@ def tile_picked_dttzmhesntwcpgf_none_p_kernel(
         two_t = load_list("two_t", two)
         for q in range(4):
             rows = x_scales[0, 4 * q : 4 * q + 4, :].bitcast(I32)
-            nc.sync.dma_start(
+            queue = nc.scalar if q < 3 else nc.sync
+            queue.dma_start(
                 x_bytes[32 * q : 32 * q + 32, :].bitcast(I32), rows.unsqueeze(0).to_broadcast([8, 4, T // 4])
             )
-        w1_w = load_words("w1_w", w1_words, nc.gpsimd)
+        warm_in = keep.tile([P, 1], F32)
+        warm_out = keep.tile([P, 1], F32)
+        nc.vector.memset(warm_in[:], 0.0)
+        nc.scalar.activation(warm_out[:], warm_in[:], ACT.Sigmoid)
+
         w2_w = load_words("w2_w", w2_words, nc.gpsimd)
-        load_w_scales(0, w1_scales, 0)
+        load_w_scales(1, w2_scales, 3, nc.gpsimd)
+        w1_w = load_words("w1_w", w1_words, nc.sync)
         x_w = load_words("x_w", x_words, nc.sync)
-        for i in range(1, 4):
-            load_w_scales(0, w1_scales, i)
         for i in range(4):
-            load_w_scales(1, w2_scales, i)
+            load_w_scales(0, w1_scales, i, nc.sync)
+        for i in range(3):
+            load_w_scales(1, w2_scales, i, nc.sync)
         n1_t = load_list("n1_t", n1)
         n2_t = load_list("n2_t", n2)
         hz_t = load_list("hz_t", hz)
@@ -114,12 +115,14 @@ def tile_picked_dttzmhesntwcpgf_none_p_kernel(
         w1_dealt = keep.tile([P, H], U32, align_bytes=64)
         w2_dealt = keep.tile([P, H], U32, align_bytes=64)
         wb_dealt = keep.tile([P, H], U8, align_bytes=64)
-        for dealt, raw, tiles in (
-            (w1_dealt, w1_w, slice(0, TILES)), (w2_dealt, w2_w, slice(0, 1)), (w2_dealt, w2_w, slice(1, TILES)),
-        ):
+        nc.vector.tensor_copy(
+            w1_dealt[:].bitcast(I32).rearrange("p (t m) -> p t m", t=PACK),
+            w1_w[:].bitcast(I32).rearrange("p (m t) -> p t m", t=PACK),
+        )
+        for tiles in (slice(0, 1), slice(1, TILES)):
             nc.scalar.copy(
-                dealt[:].rearrange("p (t m) -> p t m", t=PACK)[:, tiles, :],
-                raw[:].rearrange("p (m t) -> p t m", t=PACK)[:, tiles, :],
+                w2_dealt[:].rearrange("p (t m) -> p t m", t=PACK)[:, tiles, :],
+                w2_w[:].rearrange("p (m t) -> p t m", t=PACK)[:, tiles, :],
             )
         for engine, tiles in ((nc.gpsimd, slice(0, 1)), (nc.vector, slice(1, TILES))):
             engine.tensor_copy(

from contextlib import ExitStack

import concourse.mybir as mybir

K, T, S, H, G, W = 512, 1024, 256, 512, 2048, 128
FLOPS = 4 * 2 * K * H * S

F32 = mybir.dt.float32
BF16 = mybir.dt.bfloat16
I32 = mybir.dt.int32
U32 = mybir.dt.uint32
U16 = mybir.dt.uint16
U8 = mybir.dt.uint8
FP8X4 = mybir.dt.float8_e4m3fn_x4
ALU = mybir.AluOpType
ACT = mybir.ActivationFunctionType

P = 128
PACK = 4
TILES = H // P
WIDE = 2 * S
HALF = S // 2
BANKS = 8


def tile_picked_dttzmhesntwcpgf_none_p_kernel(
    tc, x_words, x_scales, w1_words, w1_scales, w2_words, w2_scales, sl, th, gs, d_words, d_scales,
    offs, two, n1, n2, n3, k1, k2, hz, n4, n5, n6, n7, n8, out,
):
    nc = tc.nc
    with ExitStack() as ctx:
        lists = ctx.enter_context(tc.tile_pool(name="lists", bufs=1))
        keep = ctx.enter_context(tc.tile_pool(name="keep", bufs=1))
        psum = ctx.enter_context(tc.psum_pool(name="psum", bufs=1))

        def load_list(name, dram):
            tile = lists.tile(list(dram.shape), U16, name=name)
            nc.sync.dma_start(tile[:], dram)
            return tile

        def load_words(name, dram, queue):
            tile = keep.tile([P, dram.shape[2]], U32, name=name, tag=name, align_bytes=64)
            queue.dma_start(tile[:].bitcast(I32), dram[0].rearrange("p n t -> p (n t)").bitcast(I32))
            return tile

        def load_row_values(name, dram):
            tile = keep.tile([P, PACK], F32, name=name)
            nc.sync.dma_start(tile[:], dram.rearrange("(p t) o -> p (t o)", t=PACK))
            return tile

        def gather(dst, window, offsets):
            nc.vector.tensor_copy(dst, window[:].indirect(offsets[:]))

        x_bytes = keep.tile([P, T], U8, align_bytes=64)
        w_bytes = keep.tile([P, H], U8, align_bytes=64)
        d_bytes = keep.tile([P, G], U8, align_bytes=64)

        def load_w_scales(j, scales, i, queue):
            rows = scales[0, i:16:4, :].bitcast(I32)
            queue.dma_start(
                w_bytes[4 * j + i : P : 8, :].bitcast(I32), rows.unsqueeze(1).to_broadcast([4, 4, H // 4])
            )

        offs_t = load_list("offs_t", offs)
        two_t = load_list("two_t", two)
        for q in range(4):
            rows = x_scales[0, 4 * q : 4 * q + 4, :].bitcast(I32)
            queue = nc.scalar if q < 3 else nc.sync
            queue.dma_start(
                x_bytes[32 * q : 32 * q + 32, :].bitcast(I32), rows.unsqueeze(0).to_broadcast([8, 4, T // 4])
            )
        warm_in = keep.tile([P, 1], F32)
        warm_out = keep.tile([P, 1], F32)
        nc.vector.memset(warm_in[:], 0.0)
        nc.scalar.activation(warm_out[:], warm_in[:], ACT.Sigmoid)

        w2_w = load_words("w2_w", w2_words, nc.gpsimd)
        load_w_scales(1, w2_scales, 3, nc.gpsimd)
        w1_w = load_words("w1_w", w1_words, nc.sync)
        x_w = load_words("x_w", x_words, nc.sync)
        for i in range(4):
            load_w_scales(0, w1_scales, i, nc.sync)
        for i in range(3):
            load_w_scales(1, w2_scales, i, nc.sync)
        n1_t = load_list("n1_t", n1)
        n2_t = load_list("n2_t", n2)
        hz_t = load_list("hz_t", hz)
        k1_t = load_list("k1_t", k1)
        k2_t = load_list("k2_t", k2)
        for i in range(2):
            rows = d_scales[0, i:16:2, :].bitcast(I32)
            nc.sync.dma_start(d_bytes[i:P:2, :].bitcast(I32), rows.unsqueeze(1).to_broadcast([8, 8, G // 4]))
        d_w = load_words("d_w", d_words, nc.sync)
        sl_t = load_row_values("sl_t", sl)
        th_t = load_row_values("th_t", th)
        n3_t = load_list("n3_t", n3)
        gs_t = load_row_values("gs_t", gs)
        n4_t = load_list("n4_t", n4)
        n5_t = load_list("n5_t", n5)
        n6_t = load_list("n6_t", n6)
        n7_t = load_list("n7_t", n7)
        n8_t = load_list("n8_t", n8)

        xo_bytes = keep.tile([P, S], U8, align_bytes=64)
        xt_bytes = keep.tile([P, S], U8, align_bytes=64)
        xo_w = keep.tile([P, S], U32, align_bytes=64)
        xt_w = keep.tile([P, S], U32, align_bytes=64)
        gather(xo_bytes[:], x_bytes, offs_t)
        gather(xt_bytes[:], x_bytes, two_t)
        for first in (0, HALF):
            entries = slice(first // 16, (first + HALF) // 16)
            gather(xo_w[:, first : first + HALF], x_w, offs_t[:, entries])
            gather(xt_w[:, first : first + HALF], x_w, two_t[:, entries])

        w1_dealt = keep.tile([P, H], U32, align_bytes=64)
        w2_dealt = keep.tile([P, H], U32, align_bytes=64)
        wb_dealt = keep.tile([P, H], U8, align_bytes=64)
        nc.vector.tensor_copy(
            w1_dealt[:].bitcast(I32).rearrange("p (t m) -> p t m", t=PACK),
            w1_w[:].bitcast(I32).rearrange("p (m t) -> p t m", t=PACK),
        )
        for tiles in (slice(0, 1), slice(1, TILES)):
            nc.scalar.copy(
                w2_dealt[:].rearrange("p (t m) -> p t m", t=PACK)[:, tiles, :],
                w2_w[:].rearrange("p (m t) -> p t m", t=PACK)[:, tiles, :],
            )
        for engine, tiles in ((nc.gpsimd, slice(0, 1)), (nc.vector, slice(1, TILES))):
            engine.tensor_copy(
                wb_dealt[:].rearrange("p (t m) -> p t m", t=PACK)[:, tiles, :],
                w_bytes[:].rearrange("p (m t) -> p t m", t=PACK)[:, tiles, :],
            )


        y = [keep.tile([P, S], F32, name="y%d" % t) for t in range(TILES)]
        y_pieces = [(0, 0, HALF), (0, HALF, S)] + [(t, 0, S) for t in range(1, TILES)]
        for bank, (t, first, last) in enumerate(y_pieces):
            rows = slice(t * P, (t + 1) * P)
            acc = psum.tile([P, last - first], F32, name="y_acc%d" % bank, tag="bank%d" % bank)
            nc.tensor.matmul_mx(
                acc[:], lhsT=w1_dealt[:, rows].bitcast(FP8X4), lhsT_scale=wb_dealt[:, rows],
                rhs=xo_w[:, first:last].bitcast(FP8X4), rhs_scale=xo_bytes[:, first:last], start=True, stop=False,
            )
            nc.tensor.matmul_mx(
                acc[:], lhsT=w2_dealt[:, rows].bitcast(FP8X4), lhsT_scale=wb_dealt[4:P, rows],
                rhs=xt_w[:, first:last].bitcast(FP8X4), rhs_scale=xt_bytes[:, first:last], start=False, stop=True,
            )
            if bank == 0:
                nc.scalar.copy(y[t][:, first:last], acc[:])
            else:
                nc.vector.tensor_copy(y[t][:, first:last], acc[:])

        dk_w = [keep.tile([P, H], U32, name="dk%d_w" % j, align_bytes=64) for j in range(2)]
        dk_raw = keep.tile([P, 2 * H], U8, align_bytes=64)
        xh_w = keep.tile([P, S], U32, align_bytes=64)
        xh_raw = keep.tile([P, S], U8, align_bytes=64)
        gather(xh_raw[:], x_bytes, hz_t)
        gather(xh_w[:], x_w, hz_t)
        gather(dk_raw[:, H:], d_bytes, k2_t)
        gather(dk_raw[:, :H], d_bytes, k1_t)
        dk_bytes = keep.tile([P, 2 * H], U8, align_bytes=64)
        xh_bytes = keep.tile([P, S], U8, align_bytes=64)
        for placed, raw, odd in ((xh_bytes, xh_raw, 18), (dk_bytes, dk_raw, 16)):
            nc.vector.tensor_copy(placed[:].bitcast(I32), raw[:].bitcast(I32))
            for i in range(2):
                nc.gpsimd.dma_start(placed[2 + i : P : 32, :].bitcast(I32), raw[odd + i : P : 32, :].bitcast(I32))
        gather(dk_w[1][:], d_w, k2_t)
        gather(dk_w[0][:], d_w, k1_t)

        bias = keep.tile([P, PACK], F32, tag="d_w", align_bytes=64)
        nc.vector.scalar_tensor_tensor(bias[:], sl_t[:], -1.0, th_t[:], ALU.mult, ALU.mult)

        h_acc = []
        for piece, (t, first, last) in enumerate(y_pieces):
            bank = (len(y_pieces) + piece) % BANKS
            acc = psum.tile([P, last - first], F32, name="h_acc%d" % piece, tag="bank%d" % bank)
            nc.tensor.matmul_mx(
                acc[:], lhsT=dk_w[1][:, t * P : (t + 1) * P].bitcast(FP8X4),
                lhsT_scale=dk_bytes[:, H + t * P : H + (t + 1) * P],
                rhs=xh_w[:, first:last].bitcast(FP8X4), rhs_scale=xh_bytes[:, first:last], start=True, stop=False,
            )
            h_acc.append(acc)

        ds_tags = ["ds_a", "ds_b", "ds_c", "ds_a"]
        ds2_tags = ["ds2_a", "ds2_b", "ds2_c", "ds_b"]
        sg = [keep.tile([P, S], F32, name="sg_%d" % t) for t in range(TILES)]
        z = keep.tile([P, S, PACK], BF16, align_bytes=64)
        z_w = keep.tile([P, S], U32, align_bytes=64)
        z_bytes = keep.tile([P, S], U8, align_bytes=64)
        ds, ds2 = {}, {}

        def send_ds(t, first=0, last=S):
            if first == 0:
                ds[t] = keep.tile([P, WIDE], F32, name="ds_%d" % t, tag=ds_tags[t])
            nc.scalar.activation(ds[t][:].indirect(n1_t[:, first // 16 : last // 16]), y[t][:, first:last], ACT.Copy)

        def send_ds2(t, first=0, last=S):
            if first == 0:
                ds2[t] = keep.tile([P, WIDE], F32, name="ds2_%d" % t, tag=ds2_tags[t])
            nc.scalar.activation(ds2[t][:].indirect(n2_t[:, first // 16 : last // 16]), y[t][:, first:last], ACT.Copy)

        def gate(t, first, last):
            nc.scalar.activation(
                sg[t][:, first:last], ds[t][:].indirect(n3_t[:, first // 16 : last // 16]), ACT.Sigmoid,
                bias=bias[:, t : t + 1], scale=sl_t[:, t : t + 1],
            )

        def weigh(t, first, last):
            nc.vector.scalar_tensor_tensor(
                z[:, first:last, t], ds2[t][:, first:last], gs_t[:, t : t + 1], sg[t][:, first:last],
                ALU.mult, ALU.mult,
            )

        for t, first, last in y_pieces[:-1]:
            send_ds(t, first, last)
            send_ds2(t, first, last)
        gate(0, 0, S)
        weigh(0, 0, S)
        gate(1, 0, S)
        weigh(1, 0, S)
        send_ds(3)
        gate(2, 0, S)
        weigh(2, 0, S)
        send_ds2(3)
        for first in (0, HALF):
            gate(3, first, first + HALF)
            weigh(3, first, first + HALF)
        for first in (0, HALF):
            cols = slice(first, first + HALF)
            nc.vector.quantize_mx(
                out=z_w[:, cols].bitcast(FP8X4), scales=z_bytes[:, cols],
                in_=z[:, cols, :].rearrange("p n t -> p (n t)"),
            )
        for piece, (t, first, last) in enumerate(y_pieces):
            nc.tensor.matmul_mx(
                h_acc[piece][:], lhsT=dk_w[0][:, t * P : (t + 1) * P].bitcast(FP8X4),
                lhsT_scale=dk_bytes[:, t * P : (t + 1) * P],
                rhs=z_w[:, first:last].bitcast(FP8X4), rhs_scale=z_bytes[:, first:last], start=False, stop=True,
            )

        h2 = [keep.tile([P, S], F32, name="h2_%d" % t) for t in range(TILES)]
        pa = [keep.tile([P, W], F32, name="pa_%d" % t) for t in range(TILES)]
        pb = [keep.tile([P, W], F32, name="pb_%d" % t) for t in range(TILES)]
        ra = [keep.tile([P, W], F32, name="ra_%d" % t) for t in range(TILES)]
        rb = [keep.tile([P, W], F32, name="rb_%d" % t) for t in range(TILES)]
        ub = [keep.tile([P, WIDE], F32, name="ub_%d" % t) for t in range(TILES)]
        far = [keep.tile([P, S], F32, name="far_%d" % t) for t in range(TILES)]
        res = [keep.tile([P, S], F32, name="res_%d" % t) for t in range(TILES)]
        for piece, (t, first, last) in enumerate(y_pieces):
            nc.vector.tensor_scalar(h2[t][:, first:last], h_acc[piece][:], 0.0625, None, ALU.mult)

        def pair_up(t):
            nc.scalar.activation(pa[t][:], h2[t][:].indirect(n4_t[:]), ACT.Copy)
            nc.scalar.activation(pb[t][:], h2[t][:].indirect(n5_t[:]), ACT.Copy)
            nc.vector.tensor_tensor(ra[t][:], pa[t][:], pb[t][:], ALU.subtract)
            nc.vector.tensor_tensor(rb[t][:], pa[t][:], pb[t][:], ALU.min)

        def share_out(t):
            nc.scalar.activation(ub[t][:].indirect(n6_t[:]), ra[t][:], ACT.Copy)
            nc.scalar.activation(ub[t][:].indirect(n7_t[:]), rb[t][:], ACT.Copy)

        def finish(t):
            for first, last in ((0, S - 64), (S - 64, S)) if t == TILES - 1 else ((0, S),):
                entries = n8_t[:, first // 16 : last // 16]
                nc.scalar.activation(far[t][:, first:last], ub[t][:].indirect(entries), ACT.Copy)
                nc.vector.tensor_tensor(res[t][:, first:last], ub[t][:, first:last], far[t][:, first:last], ALU.max)
                nc.sync.dma_start(out[t * P : (t + 1) * P, first:last], res[t][:, first:last])

        for step in range(TILES + 2):
            if step < TILES:
                pair_up(step)
            if 1 <= step <= TILES:
                share_out(step - 1)
            if step >= 2:
                finish(step - 2)
